import numpy as np
import ml_dtypes


def mxq(x, axis, fmt="e4m3"):
    dtype, down = {"e4m3": (ml_dtypes.float8_e4m3fn, 7), "e5m2": (ml_dtypes.float8_e5m2, 14)}[fmt]
    v = np.moveaxis(np.asarray(x, np.float32).astype(ml_dtypes.bfloat16).astype(np.float64), axis, -1)
    blocks = v.reshape(v.shape[:-1] + (-1, 32))
    amax = np.abs(blocks).max(-1, keepdims=True)
    byte = np.maximum(np.where(amax > 0, np.frexp(amax)[1] - 1 + 127, 0) - down, 1)
    scale = np.exp2(byte - 127.0)
    codes = (blocks / scale).astype(np.float32).astype(dtype).astype(np.float64)
    return np.moveaxis((codes * scale).reshape(v.shape), -1, axis)


WIDE = False


def mx_kscale(k):
    if not WIDE:
        return np.ones(k)
    levels = np.array([24, -24, 12, -12, 0])
    if k % 512:
        return np.exp2(np.random.permutation(np.resize(levels, k // 32))).repeat(32)
    a = np.empty((k // 512, 16))
    for p in range(k // 512):
        a[p, :8] = np.random.permutation(np.resize(levels, 8))
        for g in range(8):
            far = levels[np.abs(levels - a[p, g]) >= 10]
            a[p, g + 8] = far[np.random.randint(len(far))]
    return np.exp2(a.ravel()).repeat(32)


def f64(x):
    return np.asarray(x).astype(np.float64)


def striped(idx):
    return np.tile(idx.reshape(-1, 16).T, (8, 1)).astype(np.uint16)


def unstriped(offs):
    return offs[:16].T.reshape(-1).astype(np.int64)


E2M1 = np.array([0.0, 0.5, 1.0, 1.5, 2.0, 3.0, 4.0, 6.0, -0.0, -0.5, -1.0, -1.5, -2.0, -3.0, -4.0, -6.0])


def pack_weight(w, fmt):
    k, n = w.shape
    w = f64(np.asarray(w, np.float32).astype(ml_dtypes.bfloat16)).reshape(k // 32, 32, n)
    amax = np.abs(w).max(1)
    if fmt == "e4m3":
        byte = np.frexp(amax)[1] - 1 + 127 - 7
    else:
        mant, ex = np.frexp(amax / 6.0)
        byte = np.where(mant > 0.5, ex, ex - 1) + 127
    byte = np.clip(np.where(amax > 0, byte, 1), 1, 254)
    scaled = (w * np.exp2(127.0 - byte)[:, None, :]).reshape(k, n).astype(np.float32)
    by_word = np.ascontiguousarray(scaled.reshape(k // 512, 128, 4, n).transpose(0, 1, 3, 2))
    if fmt == "e4m3":
        words = by_word.astype(ml_dtypes.float8_e4m3fn).view(np.uint8)
    else:
        c = by_word.astype(ml_dtypes.float4_e2m1fn).view(np.uint8) & 0xF
        words = (c[..., 0::2] | (c[..., 1::2] << 4)).reshape(k // 512, 128, 2 * n)
    return np.ascontiguousarray(words), np.ascontiguousarray(byte.astype(np.uint8).reshape(k // 512, 16, n))


def unpack_weight(words, scales, fmt):
    g, _, n = scales.shape
    words = np.ascontiguousarray(words).reshape(g, 128, n, -1)
    if fmt == "e4m3":
        vals = words.view(ml_dtypes.float8_e4m3fn).astype(np.float64)
    else:
        nib = np.empty((g, 128, n, 4), np.uint8)
        nib[..., 0::2] = words & 0xF
        nib[..., 1::2] = words >> 4
        vals = E2M1[nib]
    vals = vals * np.repeat(np.exp2(scales.astype(np.float64) - 127.0), 8, axis=1)[..., None]
    return vals.transpose(0, 1, 3, 2).reshape(g * 512, n)


def pack_table4(v):
    words, scales = pack_weight(v, "e2m1")
    g, t = words.shape[0] // 2, v.shape[1]
    return np.ascontiguousarray(words.reshape(g, 2, 128, t, 2).transpose(0, 2, 3, 1, 4).reshape(g, 128, t, 4)), scales


def unpack_table4(words, scales):
    g, _, t, _ = words.shape
    return unpack_weight(words.reshape(g, 128, t, 2, 2).transpose(0, 3, 1, 2, 4).reshape(2 * g, 128, 2 * t), scales, "e2m1")


def planes(y):
    n, m = y.shape
    v = y.astype(np.float32).astype(ml_dtypes.bfloat16).astype(np.float64).reshape(n // 32, 32, m)
    top = np.abs(v).max(1)
    byte = np.clip(np.where(top > 0, np.frexp(top)[1] - 1 + 127 - 7, 1), 1, 254)
    codes = (v * np.exp2(127.0 - byte)[:, None, :]).reshape(n, m).astype(np.float32).astype(ml_dtypes.float8_e4m3fn).view(np.uint8)
    words = codes.reshape(n // 512, 128, 4, m).transpose(0, 1, 3, 2)
    return np.ascontiguousarray(words), np.ascontiguousarray(byte.astype(np.uint8).reshape(n // 512, 16, m))


def silu(f):
    return f / (1.0 + np.exp(-np.maximum(f, -700.0)))


K, R, N, T, J = 1024, 512, 512, 4096, 1024


def setup_inputs():
    n = np.random.standard_normal
    s = mx_kscale(K)[:, None]
    u = mx_kscale(R)[:, None]
    p_tab = pack_table4(n((K, T)) * s)
    p_wg = pack_weight(n((K, R)) / np.sqrt(K) / s, "e2m1")
    p_wu = pack_weight(n((K, R)) / np.sqrt(K) / s * u.T, "e4m3")
    p_wd = pack_weight(n((R, N)) / np.sqrt(R) / u, "e4m3")
    return {
        "tab_words": p_tab[0],
        "tab_scales": p_tab[1],
        "wg_words": p_wg[0],
        "wg_scales": p_wg[1],
        "wu_words": p_wu[0],
        "wu_scales": p_wu[1],
        "wd_words": p_wd[0],
        "wd_scales": p_wd[1],
        "gT": (n((N, T))).astype(np.float32),
        "offs": striped(np.random.permutation(T)[:J]),
    }


def reference(tab_words, tab_scales, wg_words, wg_scales, wu_words, wu_scales, wd_words, wd_scales, gT, offs):
    idx = unstriped(offs)
    tab_ = unpack_table4(tab_words, tab_scales)[:, idx]
    wg_ = unpack_weight(wg_words, wg_scales, "e2m1")
    wu_ = unpack_weight(wu_words, wu_scales, "e4m3")
    ga = wg_.T @ tab_
    ub = wu_.T @ tab_
    h = silu(ga) * ub
    h_ = mxq(h, 0, "e4m3")
    wd_ = unpack_weight(wd_words, wd_scales, "e4m3")
    y = wd_.T @ h_
    out_0 = y * f64(gT)[:, idx]
    return (out_0,) + planes(out_0)

@@ -1,0 +1,249 @@
+from contextlib import ExitStack
+
+import concourse.mybir as mybir
+
+K, R, N, T, J = 1024, 512, 512, 4096, 1024
+FLOPS = 2 * J * (2 * K * R + R * N)
+
+F32 = mybir.dt.float32
+BF16 = mybir.dt.bfloat16
+I32 = mybir.dt.int32
+U32 = mybir.dt.uint32
+U16 = mybir.dt.uint16
+U8 = mybir.dt.uint8
+FP8X4 = mybir.dt.float8_e4m3fn_x4
+FP4X4 = mybir.dt.float4_e2m1fn_x4
+MULT = mybir.AluOpType.mult
+SILU = mybir.ActivationFunctionType.Silu
+
+P = 128
+PACK = 4
+PASSES = K // (P * PACK)
+QUADS = 4
+QUARTER = J // 4
+CHUNK = 128
+STAGE0 = 96
+WD_HALF = N // PASSES
+ROW_TAB, ROW_WG, ROW_WU, ROW_WD = 0, J, J + R, J + 2 * R
+ROW = J + 2 * R + WD_HALF
+
+
+def tile_list_gmlpt_silu_gateP_kernel(
+    tc, tab_words, tab_scales, wg_words, wg_scales, wu_words, wu_scales, wd_words, wd_scales, gT, offs,
+    out_0, out_1, out_2,
+):
+    nc = tc.nc
+    with ExitStack() as ctx:
+        lists = ctx.enter_context(tc.tile_pool(name="lists", bufs=1))
+        keep = ctx.enter_context(tc.tile_pool(name="keep", bufs=1))
+        ring = ctx.enter_context(tc.tile_pool(name="ring", bufs=3))
+        psum = ctx.enter_context(tc.psum_pool(name="psum", bufs=1))
+
+        offsets = lists.tile([P, J // 16], U16, name="offsets")
+        nc.sync.dma_start(offsets[:], offs)
+
+        def listed(j0, count):
+            return offsets[:, j0 // 16 : (j0 + count) // 16]
+
+        tab_rows = keep.tile([P, T], U8, name="tab_rows", align_bytes=64)
+        w_rows = keep.tile([P, 2, R], U8, name="w_rows", align_bytes=64)
+        staged = keep.tile([P, ROW], U8, name="staged", tag="staged_then_gate", align_bytes=64)
+        planes = keep.tile([P, PASSES * ROW], U8, name="planes", align_bytes=64)
+        nc.sync.dma_start(tab_rows[STAGE0:P, :].bitcast(I32), tab_scales.rearrange("a q t -> q a t").bitcast(I32))
+        nc.sync.dma_start(w_rows[STAGE0:P, 0, :].bitcast(I32), wg_scales.rearrange("a q r -> q a r").bitcast(I32))
+        nc.sync.dma_start(w_rows[STAGE0:P, 1, :].bitcast(I32), wu_scales.rearrange("a q r -> q a r").bitcast(I32))
+        nc.sync.dma_start(
+            staged[STAGE0:P, ROW_WD:ROW].bitcast(I32),
+            wd_scales[0].rearrange("q (a n) -> (q a) n", a=PASSES).bitcast(I32),
+        )
+        nc.vector.memset(tab_rows[0:STAGE0, :].bitcast(I32), 0)
+        nc.vector.memset(w_rows[0:STAGE0].rearrange("p w r -> p (w r)").bitcast(I32), 0)
+        nc.gpsimd.memset(planes[:].bitcast(I32), 0)
+
+        wg_raw = keep.tile([P, PASSES, R // 2], I32, name="wg_raw")
+        wu_raw = keep.tile([P, PASSES, R], I32, name="wu_raw")
+        wd_raw = keep.tile([P, N], I32, name="wd_raw")
+        table = keep.tile([P, T], I32, name="table", tag="table_then_gate", align_bytes=64)
+        nc.sync.dma_start(wg_raw[:], wg_words.bitcast(I32).rearrange("a p r -> p a r"))
+        nc.sync.dma_start(wu_raw[:], wu_words.rearrange("a p r i -> p a (r i)").bitcast(I32))
+        nc.sync.dma_start(table[:], tab_words[0].rearrange("p t i -> p (t i)").bitcast(I32))
+        nc.sync.dma_start(wd_raw[:], wd_words[0].rearrange("p n i -> p (n i)").bitcast(I32))
+
+        gate_rows = gT.rearrange("(p i) t -> i p t", i=PACK)
+        gates = []
+        for i in range(2):
+            gate = keep.tile([P, T], F32, name="gate%d" % i, align_bytes=64)
+            nc.sync.dma_start(gate[:], gate_rows[i])
+            gates.append(gate)
+
+        picked_rows = keep.tile([P, J], U8, name="picked_rows", align_bytes=64)
+        nc.vector.tensor_copy(picked_rows[:], tab_rows[:].indirect(offsets[:]))
+        nc.vector.tensor_copy(staged[:, ROW_TAB:ROW_WG].bitcast(I32), picked_rows[:].bitcast(I32))
+        nc.vector.tensor_copy(
+            staged[:, ROW_WG:ROW_WD].rearrange("p (w i m) -> p w m i", w=2, i=PACK),
+            w_rows[:].rearrange("p w (m i) -> p w m i", i=PACK),
+        )
+
+        wg = keep.tile([P, PASSES, R], U16, name="wg", align_bytes=64)
+        wu = keep.tile([P, PASSES, R], U32, name="wu", align_bytes=64)
+        wd = keep.tile([P, N], U32, name="wd", align_bytes=64)
+        nc.scalar.copy(
+            wg[:].rearrange("p a (i m) -> p a m i", i=PACK),
+            wg_raw[:].bitcast(U16).rearrange("p a (m i) -> p a m i", i=PACK),
+        )
+        nc.scalar.copy(
+            wu[:].rearrange("p a (i m) -> p a m i", i=PACK),
+            wu_raw[:].bitcast(U32).rearrange("p a (m i) -> p a m i", i=PACK),
+        )
+        rows_per_quad = 4 * PASSES
+        for quad in range(QUADS):
+            first = STAGE0 + rows_per_quad * quad
+            nc.scalar.dma_start(
+                planes[32 * quad : 32 * quad + 4, :].bitcast(I32).rearrange("r (a c) -> r a c", a=PASSES),
+                staged[first : first + rows_per_quad, :].bitcast(I32),
+            )
+        nc.scalar.copy(
+            wd[:].rearrange("p (i m) -> p m i", i=PACK),
+            wd_raw[:].bitcast(U32).rearrange("p (m i) -> p m i", i=PACK),
+        )
+
+        gate = keep.tile([P, T], F32, name="gate2", tag="staged_then_gate", align_bytes=64)
+        nc.sync.dma_start(gate[:], gate_rows[2])
+        gates.append(gate)
+
+        def plane(a, first, count):
+            return planes[:, a * ROW + first : a * ROW + first + count]
+
+        parted = []
+
+        def pick_words(quarter):
+            pairs = ring.tile([P, QUARTER], U32, name="pairs", align_bytes=64)
+            nc.vector.tensor_copy(pairs[:], table[:].bitcast(U32).indirect(listed(quarter * QUARTER, QUARTER)))
+            words = keep.tile([P, PASSES, QUARTER], U16, name="words%d" % quarter, align_bytes=64)
+            nc.vector.tensor_copy(words[:], pairs[:].bitcast(U16).rearrange("p (j a) -> p a j", a=PASSES))
+            parted.append(words)
+
+        h_codes = keep.tile([P, J], U32, name="h_codes", align_bytes=64)
+        h_scales = keep.tile([P, J], U8, name="h_scales", align_bytes=64)
+        y = keep.tile([P, PACK, J], F32, name="y")
+        wd_plane = keep.tile([P, N], U8, name="wd_plane", align_bytes=64)
+
+        def first_products(chunk, h_bf16):
+            j0 = chunk * CHUNK
+            inner = j0 % QUARTER
+            words = parted[j0 // QUARTER]
+            banks = []
+            for name, weight, dtype, row in (("ga", wg, FP4X4, ROW_WG), ("ub", wu, FP8X4, ROW_WU)):
+                bank = psum.tile([P, PACK, CHUNK], F32, name=name, tag=name, bufs=3)
+                for i in range(PACK):
+                    for a in range(PASSES):
+                        nc.tensor.matmul_mx(
+                            out=bank[:, i, :],
+                            lhsT=weight[:, a, i * P : (i + 1) * P].bitcast(dtype),
+                            lhsT_scale=plane(a, row + i * P, P),
+                            rhs=words[:, a, inner : inner + CHUNK].bitcast(FP4X4),
+                            rhs_scale=plane(a, ROW_TAB + j0, CHUNK),
+                            start=(a == 0),
+                            stop=(a == PASSES - 1),
+                        )
+                banks.append(bank)
+            gated = ring.tile([P, CHUNK, PACK], F32, name="gated")
+            nc.scalar.activation(gated[:], banks[0][:].rearrange("p i j -> p j i"), SILU)
+            nc.vector.tensor_tensor(
+                h_bf16[:, inner : inner + CHUNK, :], banks[1][:].rearrange("p i j -> p j i"), gated[:], MULT
+            )
+
+        def second_product(quarter):
+            cols = slice(quarter * QUARTER, (quarter + 1) * QUARTER)
+            for pair in range(2):
+                bank = psum.tile([P, 2, QUARTER], F32, name="yb", tag="yb", bufs=2)
+                for e in range(2):
+                    i = 2 * pair + e
+                    nc.tensor.matmul_mx(
+                        out=bank[:, e, :],
+                        lhsT=wd[:, i * P : (i + 1) * P].bitcast(FP8X4),
+                        lhsT_scale=wd_plane[:, i * P : (i + 1) * P],
+                        rhs=h_codes[:, cols].bitcast(FP8X4),
+                        rhs_scale=h_scales[:, cols],
+                        start=True,
+                        stop=True,
+                    )
+                nc.scalar.copy(y[:, 2 * pair : 2 * pair + 2, cols], bank[:])
+
+        pick_words(0)
+        pick_words(1)
+        for quarter in range(4):
+            h_bf16 = ring.tile([P, QUARTER, PACK], BF16, name="h_bf16", align_bytes=64)
+            first_products(2 * quarter, h_bf16)
+            if quarter == 0:
+                nc.vector.tensor_copy(
+                    wd_plane[:].rearrange("p (i a m) -> p a m i", i=PACK, a=PASSES),
+                    planes[:].rearrange("p (a c) -> p a c", a=PASSES)[:, :, ROW_WD:ROW].rearrange(
+                        "p a (m i) -> p a m i", i=PACK
+                    ),
+                )
+            if quarter > 0:
+                second_product(quarter - 1)
+            if quarter + 2 < 4:
+                pick_words(quarter + 2)
+            first_products(2 * quarter + 1, h_bf16)
+            cols = slice(quarter * QUARTER, (quarter + 1) * QUARTER)
+            nc.vector.quantize_mx(
+                out=h_codes[:, cols].bitcast(FP8X4),
+                scales=h_scales[:, cols],
+                in_=h_bf16[:].rearrange("p j i -> p (j i)"),
+            )
+        second_product(3)
+
+        gate = keep.tile([P, T], F32, name="gate3", tag="table_then_gate", align_bytes=64)
+        nc.sync.dma_start(gate[:], gate_rows[3])
+        gates.append(gate)
+
+        result = keep.tile([P, PACK, J], F32, name="result")
+        out_rows = out_0.rearrange("(p i) j -> p i j", i=PACK)
+
+        def apply_gate(i, j0, count):
+            nc.vector.tensor_tensor(
+                result[:, i, j0 : j0 + count], gates[i][:].indirect(listed(j0, count)), y[:, i, j0 : j0 + count], MULT
+            )
+
+        for i, count in ((0, J // 4), (1, J // 2), (2, J)):
+            for j0 in range(0, J, count):
+                apply_gate(i, j0, count)
+            if i == 1:
+                nc.sync.dma_start(out_rows[:, 0:2, :], result[:, 0:2, :])
+        nc.sync.dma_start(out_rows[:, 2, :], result[:, 2, :])
+
+        o_codes = keep.tile([P, J], U32, name="o_codes", align_bytes=64)
+        o_scales = keep.tile([P, J], U8, name="o_scales", align_bytes=64)
+        words_out = out_1[0].rearrange("p j i -> p (j i)").bitcast(I32)
+
+        def hand_on(quarter):
+            cols = slice(quarter * QUARTER, (quarter + 1) * QUARTER)
+            rounded = ring.tile([P, QUARTER, PACK], BF16, name="rounded", align_bytes=64)
+            nc.scalar.copy(
+                rounded[:].rearrange("p (c e) i -> p c i e", e=4),
+                result[:, :, cols].rearrange("p i (c e) -> p c i e", e=4),
+            )
+            nc.vector.quantize_mx(
+                out=o_codes[:, cols].bitcast(FP8X4),
+                scales=o_scales[:, cols],
+                in_=rounded[:].rearrange("p j i -> p (j i)"),
+            )
+            if quarter % 2 == 1:
+                half = slice((quarter - 1) * QUARTER, (quarter + 1) * QUARTER)
+                nc.sync.dma_start(words_out[:, half], o_codes[:, half].bitcast(I32))
+
+        for quarter in range(4):
+            apply_gate(3, quarter * QUARTER, QUARTER)
+            if quarter % 2 == 1:
+                half = slice((quarter - 1) * QUARTER, (quarter + 1) * QUARTER)
+                nc.sync.dma_start(out_rows[:, 3, half], result[:, 3, half])
+            if quarter > 0:
+                hand_on(quarter - 1)
+        hand_on(3)
+        for quad in range(QUADS):
+            engine = nc.sync if quad % 2 == 0 else nc.scalar
+            engine.dma_start(
+                out_2[0, 4 * quad : 4 * quad + 4, :].bitcast(I32), o_scales[32 * quad : 32 * quad + 4, :].bitcast(I32)
+            )

@@ -37,6 +37,7 @@ def tile_list_gmlpt_silu_gateP_kernel(
         lists = ctx.enter_context(tc.tile_pool(name="lists", bufs=1))
         keep = ctx.enter_context(tc.tile_pool(name="keep", bufs=1))
         ring = ctx.enter_context(tc.tile_pool(name="ring", bufs=3))
+        reused = ctx.enter_context(tc.tile_pool(name="reused", bufs=1))
         psum = ctx.enter_context(tc.psum_pool(name="psum", bufs=1))
 
         offsets = lists.tile([P, J // 16], U16, name="offsets")
@@ -58,58 +59,57 @@ def tile_list_gmlpt_silu_gateP_kernel(
         )
         nc.vector.memset(tab_rows[0:STAGE0, :].bitcast(I32), 0)
         nc.vector.memset(w_rows[0:STAGE0].rearrange("p w r -> p (w r)").bitcast(I32), 0)
-        nc.gpsimd.memset(planes[:].bitcast(I32), 0)
+        nc.vector.memset(planes[:].bitcast(I32), 0)
 
-        wg_raw = keep.tile([P, PASSES, R // 2], I32, name="wg_raw")
-        wu_raw = keep.tile([P, PASSES, R], I32, name="wu_raw")
-        wd_raw = keep.tile([P, N], I32, name="wd_raw")
+        late_bytes = 4 * N
+        wg_raw = reused.tile([P, PASSES, R // 2], I32, name="wg_raw", offset=late_bytes - R, align_bytes=64)
         table = keep.tile([P, T], I32, name="table", tag="table_then_gate", align_bytes=64)
         nc.sync.dma_start(wg_raw[:], wg_words.bitcast(I32).rearrange("a p r -> p a r"))
-        nc.sync.dma_start(wu_raw[:], wu_words.rearrange("a p r i -> p a (r i)").bitcast(I32))
         nc.sync.dma_start(table[:], tab_words[0].rearrange("p t i -> p (t i)").bitcast(I32))
-        nc.sync.dma_start(wd_raw[:], wd_words[0].rearrange("p n i -> p (n i)").bitcast(I32))
+        wu_raw = keep.tile([P, PASSES, R], I32, name="wu_raw")
+        nc.sync.dma_start(wu_raw[:], wu_words.rearrange("a p r i -> p a (r i)").bitcast(I32))
 
         gate_rows = gT.rearrange("(p i) t -> i p t", i=PACK)
         gates = []
-        for i in range(2):
-            gate = keep.tile([P, T], F32, name="gate%d" % i, align_bytes=64)
-            nc.sync.dma_start(gate[:], gate_rows[i])
+
+        def load_gate(gate):
+            nc.sync.dma_start(gate[:], gate_rows[len(gates)])
             gates.append(gate)
 
         picked_rows = keep.tile([P, J], U8, name="picked_rows", align_bytes=64)
         nc.vector.tensor_copy(picked_rows[:], tab_rows[:].indirect(offsets[:]))
-        nc.vector.tensor_copy(staged[:, ROW_TAB:ROW_WG].bitcast(I32), picked_rows[:].bitcast(I32))
         nc.vector.tensor_copy(
             staged[:, ROW_WG:ROW_WD].rearrange("p (w i m) -> p w m i", w=2, i=PACK),
             w_rows[:].rearrange("p w (m i) -> p w m i", i=PACK),
         )
+        nc.vector.tensor_copy(staged[:, ROW_TAB:ROW_WG].bitcast(I32), picked_rows[:].bitcast(I32))
 
         wg = keep.tile([P, PASSES, R], U16, name="wg", align_bytes=64)
         wu = keep.tile([P, PASSES, R], U32, name="wu", align_bytes=64)
         wd = keep.tile([P, N], U32, name="wd", align_bytes=64)
-        nc.scalar.copy(
+        nc.vector.tensor_copy(
             wg[:].rearrange("p a (i m) -> p a m i", i=PACK),
             wg_raw[:].bitcast(U16).rearrange("p a (m i) -> p a m i", i=PACK),
-        )
-        nc.scalar.copy(
-            wu[:].rearrange("p a (i m) -> p a m i", i=PACK),
-            wu_raw[:].bitcast(U32).rearrange("p a (m i) -> p a m i", i=PACK),
         )
         rows_per_quad = 4 * PASSES
         for quad in range(QUADS):
             first = STAGE0 + rows_per_quad * quad
-            nc.scalar.dma_start(
+            nc.sync.dma_start(
                 planes[32 * quad : 32 * quad + 4, :].bitcast(I32).rearrange("r (a c) -> r a c", a=PASSES),
                 staged[first : first + rows_per_quad, :].bitcast(I32),
             )
+        for a in range(PASSES):
+            nc.scalar.copy(
+                wu[:, a, :].rearrange("p (i m) -> p m i", i=PACK),
+                wu_raw[:, a, :].bitcast(U32).rearrange("p (m i) -> p m i", i=PACK),
+            )
+        wd_raw = reused.tile([P, N], I32, name="wd_raw", offset=0, align_bytes=64)
+        nc.sync.dma_start(wd_raw[:], wd_words[0].rearrange("p n i -> p (n i)").bitcast(I32))
         nc.scalar.copy(
-            wd[:].rearrange("p (i m) -> p m i", i=PACK),
-            wd_raw[:].bitcast(U32).rearrange("p (m i) -> p m i", i=PACK),
+            wd[:].rearrange("p (i m) -> p m i", i=PACK), wd_raw[:].bitcast(U32).rearrange("p (m i) -> p m i", i=PACK)
         )
-
-        gate = keep.tile([P, T], F32, name="gate2", tag="staged_then_gate", align_bytes=64)
-        nc.sync.dma_start(gate[:], gate_rows[2])
-        gates.append(gate)
+        load_gate(reused.tile([P, T], F32, name="gate0", offset=late_bytes, align_bytes=64))
+        load_gate(keep.tile([P, T], F32, name="gate1", tag="staged_then_gate", align_bytes=64))
 
         def plane(a, first, count):
             return planes[:, a * ROW + first : a * ROW + first + count]
@@ -117,9 +117,9 @@ def tile_list_gmlpt_silu_gateP_kernel(
         parted = []
 
         def pick_words(quarter):
-            pairs = ring.tile([P, QUARTER], U32, name="pairs", align_bytes=64)
+            pairs = ring.tile([P, QUARTER], U32, name="pairs", bufs=2, align_bytes=64)
             nc.vector.tensor_copy(pairs[:], table[:].bitcast(U32).indirect(listed(quarter * QUARTER, QUARTER)))
-            words = keep.tile([P, PASSES, QUARTER], U16, name="words%d" % quarter, align_bytes=64)
+            words = keep.tile([P, PASSES, QUARTER], U16, name="words%d" % quarter, tag="words%d" % quarter, align_bytes=64)
             nc.vector.tensor_copy(words[:], pairs[:].bitcast(U16).rearrange("p (j a) -> p a j", a=PASSES))
             parted.append(words)
 
@@ -153,12 +153,25 @@ def tile_list_gmlpt_silu_gateP_kernel(
                 h_bf16[:, inner : inner + CHUNK, :], banks[1][:].rearrange("p i j -> p j i"), gated[:], MULT
             )
 
-        def second_product(quarter):
-            cols = slice(quarter * QUARTER, (quarter + 1) * QUARTER)
-            for pair in range(2):
-                bank = psum.tile([P, 2, QUARTER], F32, name="yb", tag="yb", bufs=2)
-                for e in range(2):
-                    i = 2 * pair + e
+        result = keep.tile([P, PACK, J], F32, name="result")
+        early = keep.tile([P, PACK - 1, QUARTER], F32, name="early")
+        last = J - QUARTER
+
+        def quantise_h(h_bf16, j0, count):
+            inner = j0 % QUARTER
+            nc.vector.quantize_mx(
+                out=h_codes[:, j0 : j0 + count].bitcast(FP8X4),
+                scales=h_scales[:, j0 : j0 + count],
+                in_=h_bf16[:, inner : inner + count, :].rearrange("p j i -> p (j i)"),
+            )
+
+        def second_product(j0, count):
+            cols = slice(j0, j0 + count)
+            per_bank = 512 // count
+            for first in range(0, PACK, per_bank):
+                bank = psum.tile([P, per_bank, count], F32, name="yb", tag="yb", bufs=2)
+                for e in range(per_bank):
+                    i = first + e
                     nc.tensor.matmul_mx(
                         out=bank[:, e, :],
                         lhsT=wd[:, i * P : (i + 1) * P].bitcast(FP8X4),
@@ -168,59 +181,70 @@ def tile_list_gmlpt_silu_gateP_kernel(
                         start=True,
                         stop=True,
                     )
-                nc.scalar.copy(y[:, 2 * pair : 2 * pair + 2, cols], bank[:])
-
-        pick_words(0)
-        pick_words(1)
-        for quarter in range(4):
-            h_bf16 = ring.tile([P, QUARTER, PACK], BF16, name="h_bf16", align_bytes=64)
-            first_products(2 * quarter, h_bf16)
-            if quarter == 0:
-                nc.vector.tensor_copy(
-                    wd_plane[:].rearrange("p (i a m) -> p a m i", i=PACK, a=PASSES),
-                    planes[:].rearrange("p (a c) -> p a c", a=PASSES)[:, :, ROW_WD:ROW].rearrange(
-                        "p a (m i) -> p a m i", i=PACK
-                    ),
-                )
-            if quarter > 0:
-                second_product(quarter - 1)
-            if quarter + 2 < 4:
-                pick_words(quarter + 2)
-            first_products(2 * quarter + 1, h_bf16)
-            cols = slice(quarter * QUARTER, (quarter + 1) * QUARTER)
-            nc.vector.quantize_mx(
-                out=h_codes[:, cols].bitcast(FP8X4),
-                scales=h_scales[:, cols],
-                in_=h_bf16[:].rearrange("p j i -> p (j i)"),
-            )
-        second_product(3)
-
-        gate = keep.tile([P, T], F32, name="gate3", tag="table_then_gate", align_bytes=64)
-        nc.sync.dma_start(gate[:], gate_rows[3])
-        gates.append(gate)
-
-        result = keep.tile([P, PACK, J], F32, name="result")
-        out_rows = out_0.rearrange("(p i) j -> p i j", i=PACK)
+                if j0 < last:
+                    nc.scalar.copy(y[:, first : first + per_bank, cols], bank[:])
+                else:
+                    nc.scalar.copy(y[:, PACK - 1, cols], bank[:, PACK - 1, :])
+                    nc.vector.tensor_tensor(
+                        result[:, 0 : PACK - 1, cols],
+                        bank[:, 0 : PACK - 1, :],
+                        early[:, :, j0 - last : j0 - last + count],
+                        MULT,
+                    )
 
         def apply_gate(i, j0, count):
             nc.vector.tensor_tensor(
                 result[:, i, j0 : j0 + count], gates[i][:].indirect(listed(j0, count)), y[:, i, j0 : j0 + count], MULT
             )
 
-        for i, count in ((0, J // 4), (1, J // 2), (2, J)):
-            for j0 in range(0, J, count):
+        def pick_early(i):
+            nc.vector.tensor_copy(early[:, i, :], gates[i][:].indirect(listed(last, QUARTER)))
+
+        for quarter in range(4):
+            pick_words(quarter)
+        load_gate(keep.tile([P, T], F32, name="gate2", tag="table_then_gate", align_bytes=64))
+        nc.vector.tensor_copy(
+            wd_plane[:].rearrange("p (i a m) -> p a m i", i=PACK, a=PASSES),
+            planes[:].rearrange("p (a c) -> p a c", a=PASSES)[:, :, ROW_WD:ROW].rearrange(
+                "p a (m i) -> p a m i", i=PACK
+            ),
+        )
+        for quarter in range(4):
+            j0 = quarter * QUARTER
+            h_bf16 = ring.tile([P, QUARTER, PACK], BF16, name="h_bf16", align_bytes=64)
+            first_products(2 * quarter, h_bf16)
+            if quarter > 0:
+                second_product(j0 - QUARTER, QUARTER)
+            if j0 == last:
+                quantise_h(h_bf16, j0, CHUNK)
+            first_products(2 * quarter + 1, h_bf16)
+            if quarter == 0:
+                load_gate(keep.tile([P, T], F32, name="gate3", tag="words0", align_bytes=64))
+            if j0 == last:
+                quantise_h(h_bf16, j0 + CHUNK, CHUNK)
+            else:
+                quantise_h(h_bf16, j0, QUARTER)
+        for i in range(PACK - 1):
+            pick_early(i)
+        second_product(last, CHUNK)
+        second_product(last + CHUNK, CHUNK)
+
+        out_rows = out_0.rearrange("(p i) j -> p i j", i=PACK)
+        for i, widths in ((0, (256, 256, 256)), (1, (512, 256)), (2, (768,))):
+            j0 = 0
+            for count in widths:
                 apply_gate(i, j0, count)
-            if i == 1:
-                nc.sync.dma_start(out_rows[:, 0:2, :], result[:, 0:2, :])
-        nc.sync.dma_start(out_rows[:, 2, :], result[:, 2, :])
+                j0 = j0 + count
+        nc.sync.dma_start(out_rows[:, 0 : PACK - 1, 0:last], result[:, 0 : PACK - 1, 0:last])
+        nc.sync.dma_start(out_rows[:, 0 : PACK - 1, last:J], result[:, 0 : PACK - 1, last:J])
 
         o_codes = keep.tile([P, J], U32, name="o_codes", align_bytes=64)
         o_scales = keep.tile([P, J], U8, name="o_scales", align_bytes=64)
         words_out = out_1[0].rearrange("p j i -> p (j i)").bitcast(I32)
 
-        def hand_on(quarter):
-            cols = slice(quarter * QUARTER, (quarter + 1) * QUARTER)
-            rounded = ring.tile([P, QUARTER, PACK], BF16, name="rounded", align_bytes=64)
+        def hand_on(j0, count):
+            cols = slice(j0, j0 + count)
+            rounded = ring.tile([P, count, PACK], BF16, name="rounded", align_bytes=64)
             nc.scalar.copy(
                 rounded[:].rearrange("p (c e) i -> p c i e", e=4),
                 result[:, :, cols].rearrange("p i (c e) -> p c i e", e=4),
@@ -230,18 +254,20 @@ def tile_list_gmlpt_silu_gateP_kernel(
                 scales=o_scales[:, cols],
                 in_=rounded[:].rearrange("p j i -> p (j i)"),
             )
-            if quarter % 2 == 1:
-                half = slice((quarter - 1) * QUARTER, (quarter + 1) * QUARTER)
-                nc.sync.dma_start(words_out[:, half], o_codes[:, half].bitcast(I32))
+            if j0 + count in word_stores:
+                done = slice(word_stores[j0 + count], j0 + count)
+                nc.sync.dma_start(words_out[:, done], o_codes[:, done].bitcast(I32))
 
-        for quarter in range(4):
-            apply_gate(3, quarter * QUARTER, QUARTER)
-            if quarter % 2 == 1:
-                half = slice((quarter - 1) * QUARTER, (quarter + 1) * QUARTER)
-                nc.sync.dma_start(out_rows[:, 3, half], result[:, 3, half])
-            if quarter > 0:
-                hand_on(quarter - 1)
-        hand_on(3)
+        word_stores = {512: 0, 896: 512, 1024: 896}
+        pieces = [(0, 256), (256, 256), (512, 256), (768, 128), (896, 128)]
+        for n, (j0, count) in enumerate(pieces):
+            apply_gate(PACK - 1, j0, count)
+            if (j0 + count) % 512 == 0:
+                half = slice(j0 + count - 512, j0 + count)
+                nc.sync.dma_start(out_rows[:, PACK - 1, half], result[:, PACK - 1, half])
+            if n > 0:
+                hand_on(*pieces[n - 1])
+        hand_on(*pieces[-1])
         for quad in range(QUADS):
             engine = nc.sync if quad % 2 == 0 else nc.scalar
             engine.dma_start(

from contextlib import ExitStack

import concourse.mybir as mybir

K, R, N, T, J = 1024, 512, 512, 4096, 1024
FLOPS = 2 * J * (2 * K * R + R * N)

F32 = mybir.dt.float32
BF16 = mybir.dt.bfloat16
I32 = mybir.dt.int32
U32 = mybir.dt.uint32
U16 = mybir.dt.uint16
U8 = mybir.dt.uint8
FP8X4 = mybir.dt.float8_e4m3fn_x4
FP4X4 = mybir.dt.float4_e2m1fn_x4
MULT = mybir.AluOpType.mult
SILU = mybir.ActivationFunctionType.Silu

P = 128
PACK = 4
PASSES = K // (P * PACK)
QUADS = 4
QUARTER = J // 4
CHUNK = 128
STAGE0 = 96
WD_HALF = N // PASSES
ROW_TAB, ROW_WG, ROW_WU, ROW_WD = 0, J, J + R, J + 2 * R
ROW = J + 2 * R + WD_HALF


def tile_list_gmlpt_silu_gateP_kernel(
    tc, tab_words, tab_scales, wg_words, wg_scales, wu_words, wu_scales, wd_words, wd_scales, gT, offs,
    out_0, out_1, out_2,
):
    nc = tc.nc
    with ExitStack() as ctx:
        lists = ctx.enter_context(tc.tile_pool(name="lists", bufs=1))
        keep = ctx.enter_context(tc.tile_pool(name="keep", bufs=1))
        ring = ctx.enter_context(tc.tile_pool(name="ring", bufs=3))
        reused = ctx.enter_context(tc.tile_pool(name="reused", bufs=1))
        psum = ctx.enter_context(tc.psum_pool(name="psum", bufs=1))

        offsets = lists.tile([P, J // 16], U16, name="offsets")
        nc.sync.dma_start(offsets[:], offs)

        def listed(j0, count):
            return offsets[:, j0 // 16 : (j0 + count) // 16]

        tab_rows = keep.tile([P, T], U8, name="tab_rows", align_bytes=64)
        w_rows = keep.tile([P, 2, R], U8, name="w_rows", align_bytes=64)
        staged = keep.tile([P, ROW], U8, name="staged", tag="staged_then_gate", align_bytes=64)
        planes = keep.tile([P, PASSES * ROW], U8, name="planes", align_bytes=64)
        nc.sync.dma_start(tab_rows[STAGE0:P, :].bitcast(I32), tab_scales.rearrange("a q t -> q a t").bitcast(I32))
        nc.sync.dma_start(w_rows[STAGE0:P, 0, :].bitcast(I32), wg_scales.rearrange("a q r -> q a r").bitcast(I32))
        nc.sync.dma_start(w_rows[STAGE0:P, 1, :].bitcast(I32), wu_scales.rearrange("a q r -> q a r").bitcast(I32))
        nc.sync.dma_start(
            staged[STAGE0:P, ROW_WD:ROW].bitcast(I32),
            wd_scales[0].rearrange("q (a n) -> (q a) n", a=PASSES).bitcast(I32),
        )
        nc.vector.memset(tab_rows[0:STAGE0, :].bitcast(I32), 0)
        nc.vector.memset(w_rows[0:STAGE0].rearrange("p w r -> p (w r)").bitcast(I32), 0)
        nc.vector.memset(planes[:].bitcast(I32), 0)

        late_bytes = 4 * N
        wg_raw = reused.tile([P, PASSES, R // 2], I32, name="wg_raw", offset=late_bytes - R, align_bytes=64)
        table = keep.tile([P, T], I32, name="table", tag="table_then_gate", align_bytes=64)
        nc.sync.dma_start(wg_raw[:], wg_words.bitcast(I32).rearrange("a p r -> p a r"))
        nc.sync.dma_start(table[:], tab_words[0].rearrange("p t i -> p (t i)").bitcast(I32))
        wu_raw = keep.tile([P, PASSES, R], I32, name="wu_raw")
        nc.sync.dma_start(wu_raw[:], wu_words.rearrange("a p r i -> p a (r i)").bitcast(I32))

        gate_rows = gT.rearrange("(p i) t -> i p t", i=PACK)
        gates = []

        def load_gate(gate):
            nc.sync.dma_start(gate[:], gate_rows[len(gates)])
            gates.append(gate)

        picked_rows = keep.tile([P, J], U8, name="picked_rows", align_bytes=64)
        nc.vector.tensor_copy(picked_rows[:], tab_rows[:].indirect(offsets[:]))
        nc.vector.tensor_copy(
            staged[:, ROW_WG:ROW_WD].rearrange("p (w i m) -> p w m i", w=2, i=PACK),
            w_rows[:].rearrange("p w (m i) -> p w m i", i=PACK),
        )
        nc.vector.tensor_copy(staged[:, ROW_TAB:ROW_WG].bitcast(I32), picked_rows[:].bitcast(I32))

        wg = keep.tile([P, PASSES, R], U16, name="wg", align_bytes=64)
        wu = keep.tile([P, PASSES, R], U32, name="wu", align_bytes=64)
        wd = keep.tile([P, N], U32, name="wd", align_bytes=64)
        nc.vector.tensor_copy(
            wg[:].rearrange("p a (i m) -> p a m i", i=PACK),
            wg_raw[:].bitcast(U16).rearrange("p a (m i) -> p a m i", i=PACK),
        )
        rows_per_quad = 4 * PASSES
        for quad in range(QUADS):
            first = STAGE0 + rows_per_quad * quad
            nc.sync.dma_start(
                planes[32 * quad : 32 * quad + 4, :].bitcast(I32).rearrange("r (a c) -> r a c", a=PASSES),
                staged[first : first + rows_per_quad, :].bitcast(I32),
            )
        for a in range(PASSES):
            nc.scalar.copy(
                wu[:, a, :].rearrange("p (i m) -> p m i", i=PACK),
                wu_raw[:, a, :].bitcast(U32).rearrange("p (m i) -> p m i", i=PACK),
            )
        wd_raw = reused.tile([P, N], I32, name="wd_raw", offset=0, align_bytes=64)
        nc.sync.dma_start(wd_raw[:], wd_words[0].rearrange("p n i -> p (n i)").bitcast(I32))
        nc.scalar.copy(
            wd[:].rearrange("p (i m) -> p m i", i=PACK), wd_raw[:].bitcast(U32).rearrange("p (m i) -> p m i", i=PACK)
        )
        load_gate(reused.tile([P, T], F32, name="gate0", offset=late_bytes, align_bytes=64))
        load_gate(keep.tile([P, T], F32, name="gate1", tag="staged_then_gate", align_bytes=64))

        def plane(a, first, count):
            return planes[:, a * ROW + first : a * ROW + first + count]

        parted = []

        def pick_words(quarter):
            pairs = ring.tile([P, QUARTER], U32, name="pairs", bufs=2, align_bytes=64)
            nc.vector.tensor_copy(pairs[:], table[:].bitcast(U32).indirect(listed(quarter * QUARTER, QUARTER)))
            words = keep.tile([P, PASSES, QUARTER], U16, name="words%d" % quarter, tag="words%d" % quarter, align_bytes=64)
            nc.vector.tensor_copy(words[:], pairs[:].bitcast(U16).rearrange("p (j a) -> p a j", a=PASSES))
            parted.append(words)

        h_codes = keep.tile([P, J], U32, name="h_codes", align_bytes=64)
        h_scales = keep.tile([P, J], U8, name="h_scales", align_bytes=64)
        y = keep.tile([P, PACK, J], F32, name="y")
        wd_plane = keep.tile([P, N], U8, name="wd_plane", align_bytes=64)

        def first_products(chunk, h_bf16):
            j0 = chunk * CHUNK
            inner = j0 % QUARTER
            words = parted[j0 // QUARTER]
            banks = []
            for name, weight, dtype, row in (("ga", wg, FP4X4, ROW_WG), ("ub", wu, FP8X4, ROW_WU)):
                bank = psum.tile([P, PACK, CHUNK], F32, name=name, tag=name, bufs=3)
                for i in range(PACK):
                    for a in range(PASSES):
                        nc.tensor.matmul_mx(
                            out=bank[:, i, :],
                            lhsT=weight[:, a, i * P : (i + 1) * P].bitcast(dtype),
                            lhsT_scale=plane(a, row + i * P, P),
                            rhs=words[:, a, inner : inner + CHUNK].bitcast(FP4X4),
                            rhs_scale=plane(a, ROW_TAB + j0, CHUNK),
                            start=(a == 0),
                            stop=(a == PASSES - 1),
                        )
                banks.append(bank)
            gated = ring.tile([P, CHUNK, PACK], F32, name="gated")
            nc.scalar.activation(gated[:], banks[0][:].rearrange("p i j -> p j i"), SILU)
            nc.vector.tensor_tensor(
                h_bf16[:, inner : inner + CHUNK, :], banks[1][:].rearrange("p i j -> p j i"), gated[:], MULT
            )

        result = keep.tile([P, PACK, J], F32, name="result")
        early = keep.tile([P, PACK - 1, QUARTER], F32, name="early")
        last = J - QUARTER

        def quantise_h(h_bf16, j0, count):
            inner = j0 % QUARTER
            nc.vector.quantize_mx(
                out=h_codes[:, j0 : j0 + count].bitcast(FP8X4),
                scales=h_scales[:, j0 : j0 + count],
                in_=h_bf16[:, inner : inner + count, :].rearrange("p j i -> p (j i)"),
            )

        def second_product(j0, count):
            cols = slice(j0, j0 + count)
            per_bank = 512 // count
            for first in range(0, PACK, per_bank):
                bank = psum.tile([P, per_bank, count], F32, name="yb", tag="yb", bufs=2)
                for e in range(per_bank):
                    i = first + e
                    nc.tensor.matmul_mx(
                        out=bank[:, e, :],
                        lhsT=wd[:, i * P : (i + 1) * P].bitcast(FP8X4),
                        lhsT_scale=wd_plane[:, i * P : (i + 1) * P],
                        rhs=h_codes[:, cols].bitcast(FP8X4),
                        rhs_scale=h_scales[:, cols],
                        start=True,
                        stop=True,
                    )
                if j0 < last:
                    nc.scalar.copy(y[:, first : first + per_bank, cols], bank[:])
                else:
                    nc.scalar.copy(y[:, PACK - 1, cols], bank[:, PACK - 1, :])
                    nc.vector.tensor_tensor(
                        result[:, 0 : PACK - 1, cols],
                        bank[:, 0 : PACK - 1, :],
                        early[:, :, j0 - last : j0 - last + count],
                        MULT,
                    )

        def apply_gate(i, j0, count):
            nc.vector.tensor_tensor(
                result[:, i, j0 : j0 + count], gates[i][:].indirect(listed(j0, count)), y[:, i, j0 : j0 + count], MULT
            )

        def pick_early(i):
            nc.vector.tensor_copy(early[:, i, :], gates[i][:].indirect(listed(last, QUARTER)))

        for quarter in range(4):
            pick_words(quarter)
        load_gate(keep.tile([P, T], F32, name="gate2", tag="table_then_gate", align_bytes=64))
        nc.vector.tensor_copy(
            wd_plane[:].rearrange("p (i a m) -> p a m i", i=PACK, a=PASSES),
            planes[:].rearrange("p (a c) -> p a c", a=PASSES)[:, :, ROW_WD:ROW].rearrange(
                "p a (m i) -> p a m i", i=PACK
            ),
        )
        for quarter in range(4):
            j0 = quarter * QUARTER
            h_bf16 = ring.tile([P, QUARTER, PACK], BF16, name="h_bf16", align_bytes=64)
            first_products(2 * quarter, h_bf16)
            if quarter > 0:
                second_product(j0 - QUARTER, QUARTER)
            if j0 == last:
                quantise_h(h_bf16, j0, CHUNK)
            first_products(2 * quarter + 1, h_bf16)
            if quarter == 0:
                load_gate(keep.tile([P, T], F32, name="gate3", tag="words0", align_bytes=64))
            if j0 == last:
                quantise_h(h_bf16, j0 + CHUNK, CHUNK)
            else:
                quantise_h(h_bf16, j0, QUARTER)
        for i in range(PACK - 1):
            pick_early(i)
        second_product(last, CHUNK)
        second_product(last + CHUNK, CHUNK)

        out_rows = out_0.rearrange("(p i) j -> p i j", i=PACK)
        for i, widths in ((0, (256, 256, 256)), (1, (512, 256)), (2, (768,))):
            j0 = 0
            for count in widths:
                apply_gate(i, j0, count)
                j0 = j0 + count
        nc.sync.dma_start(out_rows[:, 0 : PACK - 1, 0:last], result[:, 0 : PACK - 1, 0:last])
        nc.sync.dma_start(out_rows[:, 0 : PACK - 1, last:J], result[:, 0 : PACK - 1, last:J])

        o_codes = keep.tile([P, J], U32, name="o_codes", align_bytes=64)
        o_scales = keep.tile([P, J], U8, name="o_scales", align_bytes=64)
        words_out = out_1[0].rearrange("p j i -> p (j i)").bitcast(I32)

        def hand_on(j0, count):
            cols = slice(j0, j0 + count)
            rounded = ring.tile([P, count, PACK], BF16, name="rounded", align_bytes=64)
            nc.scalar.copy(
                rounded[:].rearrange("p (c e) i -> p c i e", e=4),
                result[:, :, cols].rearrange("p i (c e) -> p c i e", e=4),
            )
            nc.vector.quantize_mx(
                out=o_codes[:, cols].bitcast(FP8X4),
                scales=o_scales[:, cols],
                in_=rounded[:].rearrange("p j i -> p (j i)"),
            )
            if j0 + count in word_stores:
                done = slice(word_stores[j0 + count], j0 + count)
                nc.sync.dma_start(words_out[:, done], o_codes[:, done].bitcast(I32))

        word_stores = {512: 0, 896: 512, 1024: 896}
        pieces = [(0, 256), (256, 256), (512, 256), (768, 128), (896, 128)]
        for n, (j0, count) in enumerate(pieces):
            apply_gate(PACK - 1, j0, count)
            if (j0 + count) % 512 == 0:
                half = slice(j0 + count - 512, j0 + count)
                nc.sync.dma_start(out_rows[:, PACK - 1, half], result[:, PACK - 1, half])
            if n > 0:
                hand_on(*pieces[n - 1])
        hand_on(*pieces[-1])
        for quad in range(QUADS):
            engine = nc.sync if quad % 2 == 0 else nc.scalar
            engine.dma_start(
                out_2[0, 4 * quad : 4 * quad + 4, :].bitcast(I32), o_scales[32 * quad : 32 * quad + 4, :].bitcast(I32)
            )
